import numpy as np
import ml_dtypes


def mxq(x, axis, fmt="e4m3"):
    dtype, down = {"e4m3": (ml_dtypes.float8_e4m3fn, 7), "e5m2": (ml_dtypes.float8_e5m2, 14)}[fmt]
    v = np.moveaxis(np.asarray(x, np.float32).astype(ml_dtypes.bfloat16).astype(np.float64), axis, -1)
    blocks = v.reshape(v.shape[:-1] + (-1, 32))
    amax = np.abs(blocks).max(-1, keepdims=True)
    byte = np.maximum(np.where(amax > 0, np.frexp(amax)[1] - 1 + 127, 0) - down, 1)
    scale = np.exp2(byte - 127.0)
    codes = (blocks / scale).astype(np.float32).astype(dtype).astype(np.float64)
    return np.moveaxis((codes * scale).reshape(v.shape), -1, axis)


WIDE = False


def mx_kscale(k):
    if not WIDE:
        return np.ones(k)
    levels = np.array([10, -10, 5, -5, 0])
    if k % 512:
        return np.exp2(np.random.permutation(np.resize(levels, k // 32))).repeat(32)
    a = np.empty((k // 512, 16))
    for p in range(k // 512):
        a[p, :8] = np.random.permutation(np.resize(levels, 8))
        for g in range(8):
            far = levels[np.abs(levels - a[p, g]) >= 10]
            a[p, g + 8] = far[np.random.randint(len(far))]
    return np.exp2(a.ravel()).repeat(32)


def f64(x):
    return np.asarray(x).astype(np.float64)


def striped8(idx):
    return np.asarray(idx).reshape(8, -1, 16).transpose(0, 2, 1).reshape(128, -1).astype(np.uint16)


def unstriped8(offs):
    return offs.reshape(8, 16, -1).transpose(0, 2, 1).reshape(8, -1).astype(np.int64)


def pick8(x, idx, run):
    r = np.arange(len(x))
    return x[r[:, None], idx[r % (8 * run) // run]]


E2M1 = np.array([0.0, 0.5, 1.0, 1.5, 2.0, 3.0, 4.0, 6.0, -0.0, -0.5, -1.0, -1.5, -2.0, -3.0, -4.0, -6.0])


def pack_weight(w, fmt):
    k, n = w.shape
    w = f64(np.asarray(w, np.float32).astype(ml_dtypes.bfloat16)).reshape(k // 32, 32, n)
    amax = np.abs(w).max(1)
    if fmt == "e4m3":
        byte = np.frexp(amax)[1] - 1 + 127 - 7
    else:
        mant, ex = np.frexp(amax / 6.0)
        byte = np.where(mant > 0.5, ex, ex - 1) + 127
    byte = np.clip(np.where(amax > 0, byte, 1), 1, 254)
    scaled = (w * np.exp2(127.0 - byte)[:, None, :]).reshape(k, n).astype(np.float32)
    by_word = np.ascontiguousarray(scaled.reshape(k // 512, 128, 4, n).transpose(0, 1, 3, 2))
    if fmt == "e4m3":
        words = by_word.astype(ml_dtypes.float8_e4m3fn).view(np.uint8)
    else:
        c = by_word.astype(ml_dtypes.float4_e2m1fn).view(np.uint8) & 0xF
        words = (c[..., 0::2] | (c[..., 1::2] << 4)).reshape(k // 512, 128, 2 * n)
    return np.ascontiguousarray(words), np.ascontiguousarray(byte.astype(np.uint8).reshape(k // 512, 16, n))


def unpack_weight(words, scales, fmt):
    g, _, n = scales.shape
    words = np.ascontiguousarray(words).reshape(g, 128, n, -1)
    if fmt == "e4m3":
        vals = words.view(ml_dtypes.float8_e4m3fn).astype(np.float64)
    else:
        nib = np.empty((g, 128, n, 4), np.uint8)
        nib[..., 0::2] = words & 0xF
        nib[..., 1::2] = words >> 4
        vals = E2M1[nib]
    vals = vals * np.repeat(np.exp2(scales.astype(np.float64) - 127.0), 8, axis=1)[..., None]
    return vals.transpose(0, 1, 3, 2).reshape(g * 512, n)


def sigmoid(v):
    return 1.0 / (1.0 + np.exp(-v))


D, K, T, U, X, I, Q = 512, 512, 1024, 1024, 1024, 512, 128


def setup_inputs():
    n = np.random.standard_normal
    idx = np.stack([np.random.permutation(U)[:I] for _ in range(8)])
    idx2 = np.stack([np.random.permutation(T)[:I] for _ in range(8)])
    idx3 = np.stack([np.random.permutation(T)[:I] for _ in range(8)])
    idx4 = np.stack([np.random.permutation(U)[:I] for _ in range(8)])
    idx5 = np.stack([np.random.permutation(X)[:I] for _ in range(8)])
    idx6 = np.stack([np.random.permutation(X)[:I] for _ in range(8)])
    fd = mx_kscale(D)
    fk = mx_kscale(K)
    wqp = pack_weight(n((D, K)) * 1.0 / np.sqrt(D) * fd[:, None] * fk, "e4m3")
    cachep = pack_weight(n((K, T)) * 1.0 / np.sqrt(K) / fk[:, None], "e2m1")
    draftp = pack_weight(n((K, U)) * 1.0 / np.sqrt(K) / fk[:, None], "e4m3")
    archp = pack_weight(n((D, X)) * 1.0 / np.sqrt(D) * fd[:, None], "e2m1")
    return {
        "states": (n((D, Q)) * 0.95 / fd[:, None]).astype(np.float32),
        "wq_words": wqp[0],
        "wq_scales": wqp[1],
        "cache_words": cachep[0],
        "cache_scales": cachep[1],
        "draft_words": draftp[0],
        "draft_scales": draftp[1],
        "arch_words": archp[0],
        "arch_scales": archp[1],
        "offs": striped8(idx),
        "offs2": striped8(idx2),
        "offs3": striped8(idx3),
        "offs4": striped8(idx4),
        "offs5": striped8(idx5),
        "offs6": striped8(idx6),
    }


def reference(states, wq_words, wq_scales, cache_words, cache_scales, draft_words, draft_scales, arch_words, arch_scales, offs, offs2, offs3, offs4, offs5, offs6):
    idx = unstriped8(offs)
    idx2 = unstriped8(offs2)
    idx3 = unstriped8(offs3)
    idx4 = unstriped8(offs4)
    idx5 = unstriped8(offs5)
    idx6 = unstriped8(offs6)
    wqu = unpack_weight(wq_words, wq_scales, "e4m3")
    cacheu = unpack_weight(cache_words, cache_scales, "e2m1")
    draftu = unpack_weight(draft_words, draft_scales, "e4m3")
    archu = unpack_weight(arch_words, arch_scales, "e2m1")
    statesq = mxq(f64(states), 0, "e4m3")
    qv = wqu.T @ statesq
    qvq = mxq(qv, 0, "e4m3")
    a = qvq.T @ cacheu
    b = qvq.T @ draftu
    c0 = statesq.T @ archu
    f1 = np.zeros((Q, T))
    f1[np.arange(Q)[:, None], idx2[np.arange(Q) % 128 // 16]] = pick8(b, idx, 16)
    sg = sigmoid(f1 * 2.0)
    mg = a * sg
    w = np.maximum(pick8(mg, idx3, 16), pick8(b, idx4, 16))
    f2 = np.zeros((Q, X))
    f2[np.arange(Q)[:, None], idx5[np.arange(Q) % 128 // 16]] = w
    cc = c0 - f2
    y = pick8(cc, idx6, 16) + pick8(mg, idx3, 16)
    return y

@@ -1,0 +1,188 @@
+from contextlib import ExitStack
+
+import concourse.mybir as mybir
+
+D, K, T, U, X, I, Q = 512, 512, 1024, 1024, 1024, 512, 128
+FLOPS = 2 * (D * K * Q + K * Q * T + K * Q * U + D * Q * X)
+
+F32 = mybir.dt.float32
+BF16 = mybir.dt.bfloat16
+I32 = mybir.dt.int32
+U32 = mybir.dt.uint32
+U16 = mybir.dt.uint16
+U8 = mybir.dt.uint8
+FP8X4 = mybir.dt.float8_e4m3fn_x4
+FP4X4 = mybir.dt.float4_e2m1fn_x4
+COPY = mybir.ActivationFunctionType.Copy
+TANH = mybir.ActivationFunctionType.Tanh
+ALU = mybir.AluOpType
+
+P = 128
+PACK = 4
+BANK = 512
+PIECE = 256
+HALF = I // 2
+LCOL = HALF // 16
+
+
+def load_scale_rows(nc, plane, scales):
+    rows = scales[0].bitcast(I32)
+    words = plane[:].bitcast(I32)
+    for r in range(4):
+        nc.sync.dma_start(words[r:P:32, :], rows[r:16:4, :])
+
+
+def tile_attend_gatedpage_sidethree_kernel(
+    tc, states, wq_words, wq_scales, cache_words, cache_scales, draft_words, draft_scales,
+    arch_words, arch_scales, offs, offs2, offs3, offs4, offs5, offs6, out,
+):
+    nc = tc.nc
+    with ExitStack() as ctx:
+        sb = ctx.enter_context(tc.tile_pool(name="sb", bufs=1))
+        ps = ctx.enter_context(tc.psum_pool(name="ps", bufs=1))
+
+        wq_plane = sb.tile([P, K], U8, name="wq_plane", align_bytes=64)
+        draft_plane = sb.tile([P, U], U8, name="draft_plane", align_bytes=64)
+        arch_plane = sb.tile([P, X], U8, name="arch_plane", align_bytes=64)
+        cache_plane = sb.tile([P, T], U8, name="cache_plane", align_bytes=64)
+        for plane in (wq_plane, draft_plane, cache_plane, arch_plane):
+            nc.gpsimd.memset(plane[:].bitcast(I32), 0)
+        f1 = sb.tile([P, T], F32, name="f1")
+        nc.gpsimd.memset(f1[:], 0.0)
+
+        s_raw = sb.tile([P, PACK, Q], F32, name="s_raw", align_bytes=256)
+        wq_raw = sb.tile([P, K], U32, name="wq_raw", tag="wq_raw_f2", align_bytes=256)
+        draft_w = sb.tile([P, U], I32, name="draft_w", align_bytes=256)
+        arch_w = sb.tile([P, 2 * X], U8, name="arch_w", align_bytes=256)
+        cache_w = sb.tile([P, 2 * T], U8, name="cache_w", align_bytes=256)
+        lists = [sb.tile([P, I // 16], U16, name="list%d" % n) for n in range(6)]
+        l1, l2, l3, l4, l5, l6 = lists
+
+        wq_stage = sb.tile([4, 4, K // 4], I32, name="wq_stage")
+        nc.sync.dma_start(wq_stage[:], wq_scales[0].bitcast(I32).rearrange("(g r) c -> r g c", r=4))
+        nc.sync.dma_start(s_raw[:], states.rearrange("(p j) q -> p j q", j=PACK))
+        nc.sync.dma_start(wq_raw[:].bitcast(I32), wq_words[0].rearrange("p n t -> p (n t)").bitcast(I32))
+        load_scale_rows(nc, draft_plane, draft_scales)
+        nc.sync.dma_start(draft_w[:], draft_words[0].rearrange("p n t -> p (n t)").bitcast(I32))
+        nc.sync.dma_start(l1[:], offs)
+        nc.sync.dma_start(l2[:], offs2)
+        load_scale_rows(nc, cache_plane, cache_scales)
+        nc.sync.dma_start(cache_w[:].bitcast(I32), cache_words[0].bitcast(I32))
+        nc.sync.dma_start(l4[:], offs4)
+        nc.sync.dma_start(l3[:], offs3)
+        load_scale_rows(nc, arch_plane, arch_scales)
+        nc.sync.dma_start(arch_w[:].bitcast(I32), arch_words[0].bitcast(I32))
+        nc.sync.dma_start(l5[:], offs5)
+        nc.sync.dma_start(l6[:], offs6)
+
+        s_bf = sb.tile([P, Q, PACK], BF16, name="s_bf", align_bytes=64)
+        nc.scalar.activation(
+            s_bf[:].rearrange("p (c i) j -> p c j i", i=4),
+            s_raw[:].rearrange("p j (c i) -> p c j i", i=4),
+            COPY,
+        )
+        for g in range(4):
+            nc.vector.tensor_copy(wq_plane[32 * g : 32 * g + 4, :].bitcast(I32), wq_stage[:, g, :])
+        wq_deal_plane = sb.tile([P, K], U8, name="wq_deal_plane", align_bytes=64)
+        nc.vector.tensor_copy(
+            wq_deal_plane[:].rearrange("p (t m) -> p t m", t=PACK),
+            wq_plane[:].rearrange("p (m t) -> p t m", t=PACK),
+        )
+        s_codes = sb.tile([P, Q], U32, name="s_codes", align_bytes=64)
+        s_plane = sb.tile([P, Q], U8, name="s_plane", align_bytes=64)
+        nc.vector.quantize_mx(s_codes[:].bitcast(FP8X4), s_plane[:], s_bf[:].rearrange("p q j -> p (q j)"))
+        wq_deal = sb.tile([P, K], U32, name="wq_deal", align_bytes=64)
+        nc.scalar.copy(
+            wq_deal[:].rearrange("p (t c i) -> p c t i", t=PACK, i=4),
+            wq_raw[:].rearrange("p (c i t) -> p c t i", t=PACK, i=4),
+        )
+
+        f2 = sb.tile([P, X], F32, name="f2", tag="wq_raw_f2", align_bytes=256)
+        nc.vector.memset(f2[:], 0.0)
+
+        qv_ps = ps.tile([P, PACK, Q], F32, name="qv_ps", tag="first")
+        for t in range(PACK):
+            cols = slice(t * P, (t + 1) * P)
+            nc.tensor.matmul_mx(
+                qv_ps[:, t, :], lhsT=wq_deal[:, cols].bitcast(FP8X4), lhsT_scale=wq_deal_plane[:, cols],
+                rhs=s_codes[:].bitcast(FP8X4), rhs_scale=s_plane[:], start=True, stop=True,
+            )
+
+        q_bf = sb.tile([P, Q, PACK], BF16, name="q_bf", align_bytes=64)
+        nc.scalar.activation(q_bf[:], qv_ps[:].rearrange("p t q -> p q t"), COPY)
+        q_codes = sb.tile([P, Q], U32, name="q_codes", align_bytes=64)
+        q_plane = sb.tile([P, Q], U8, name="q_plane", align_bytes=64)
+        nc.vector.quantize_mx(q_codes[:].bitcast(FP8X4), q_plane[:], q_bf[:].rearrange("p q t -> p (q t)"))
+
+        b = sb.tile([P, U], F32, name="b")
+        for n in range(U // PIECE):
+            cols = slice(n * PIECE, (n + 1) * PIECE)
+            b_ps = ps.tile([P, PIECE], F32, name="b_ps%d" % n, tag="b%d" % n)
+            nc.tensor.matmul_mx(
+                b_ps[:], lhsT=q_codes[:].bitcast(FP8X4), lhsT_scale=q_plane[:],
+                rhs=draft_w[:, cols].bitcast(FP8X4), rhs_scale=draft_plane[:, cols], start=True, stop=True,
+            )
+            if n % 2 == 0:
+                nc.scalar.activation(b[:, cols], b_ps[:], COPY)
+            else:
+                nc.vector.tensor_copy(b[:, cols], b_ps[:])
+        a_ps = [
+            ps.tile([P, BANK], F32, name="a_ps0", tag="b1"),
+            ps.tile([P, BANK], F32, name="a_ps1", tag="b3"),
+        ]
+        for n, bank in enumerate(a_ps):
+            nc.tensor.matmul_mx(
+                bank[:], lhsT=q_codes[:].bitcast(FP8X4), lhsT_scale=q_plane[:],
+                rhs=cache_w[:, 2 * n * BANK : 2 * (n + 1) * BANK].bitcast(FP4X4),
+                rhs_scale=cache_plane[:, n * BANK : (n + 1) * BANK], start=True, stop=True,
+            )
+
+        c0_ps = [ps.tile([P, BANK], F32, name="c0_ps%d" % n) for n in range(X // BANK)]
+        for n, bank in enumerate(c0_ps):
+            nc.tensor.matmul_mx(
+                bank[:], lhsT=s_codes[:].bitcast(FP8X4), lhsT_scale=s_plane[:],
+                rhs=arch_w[:, 2 * n * BANK : 2 * (n + 1) * BANK].bitcast(FP4X4),
+                rhs_scale=arch_plane[:, n * BANK : (n + 1) * BANK], start=True, stop=True,
+            )
+
+        halves = [(slice(h * HALF, (h + 1) * HALF), slice(h * LCOL, (h + 1) * LCOL)) for h in range(2)]
+
+        b1 = sb.tile([P, I], F32, name="b1")
+        for slots, lc in halves:
+            nc.vector.tensor_copy(b1[:, slots], b[:].indirect(l1[:, lc]))
+            nc.scalar.activation(f1[:].indirect(l2[:, lc]), b1[:, slots], COPY)
+
+        a_half = sb.tile([P, T], F32, name="a_half")
+        for n, bank in enumerate(a_ps):
+            nc.vector.tensor_scalar(a_half[:, n * BANK : (n + 1) * BANK], bank[:], 0.5, None, ALU.mult)
+        b4 = sb.tile([P, I], F32, name="b4")
+        nc.vector.tensor_copy(b4[:], b[:].indirect(l4[:]))
+
+        th = sb.tile([P, T], F32, name="th")
+        mg = sb.tile([P, T], F32, name="mg")
+        for n in range(T // PIECE):
+            cols = slice(n * PIECE, (n + 1) * PIECE)
+            nc.scalar.activation(th[:, cols], f1[:, cols], TANH)
+            nc.vector.scalar_tensor_tensor(mg[:, cols], th[:, cols], 1.0, a_half[:, cols], ALU.add, ALU.mult)
+
+        m3_lo = sb.tile([P, HALF], F32, name="m3_lo")
+        m3 = [m3_lo[:], b4[:, 0:HALF]]
+        w = sb.tile([P, I], F32, name="w")
+        for (slots, lc), m3_h in zip(halves, m3):
+            nc.vector.tensor_copy(m3_h, mg[:].indirect(l3[:, lc]))
+            nc.vector.tensor_tensor(w[:, slots], m3_h, b4[:, slots], ALU.max)
+            nc.scalar.activation(f2[:].indirect(l5[:, lc]), w[:, slots], COPY)
+
+        cc = sb.tile([P, X], F32, name="cc")
+        for n, bank in enumerate(c0_ps):
+            cols = slice(n * BANK, (n + 1) * BANK)
+            nc.vector.tensor_tensor(cc[:, cols], bank[:], f2[:, cols], ALU.subtract)
+
+        y = sb.tile([P, I], F32, name="y", align_bytes=256)
+        c6 = sb.tile([P, HALF], F32, name="c6")
+        (lo, lo_lc), (hi, hi_lc) = halves
+        nc.scalar.activation(c6[:], cc[:].indirect(l6[:, hi_lc]), COPY)
+        nc.vector.tensor_tensor(y[:, lo], cc[:].indirect(l6[:, lo_lc]), m3[0], ALU.add)
+        nc.sync.dma_start(out[:, lo], y[:, lo])
+        nc.vector.tensor_tensor(y[:, hi], c6[:], m3[1], ALU.add)
+        nc.scalar.dma_start(out[:, hi], y[:, hi])

@@ -25,11 +25,11 @@ HALF = I // 2
 LCOL = HALF // 16
 
 
-def load_scale_rows(nc, plane, scales):
+def load_scale_rows(queue, plane, scales):
     rows = scales[0].bitcast(I32)
     words = plane[:].bitcast(I32)
     for r in range(4):
-        nc.sync.dma_start(words[r:P:32, :], rows[r:16:4, :])
+        queue.dma_start(words[r:P:32, :], rows[r:16:4, :])
 
 
 def tile_attend_gatedpage_sidethree_kernel(
@@ -42,35 +42,39 @@ def tile_attend_gatedpage_sidethree_kernel(
         ps = ctx.enter_context(tc.psum_pool(name="ps", bufs=1))
 
         wq_plane = sb.tile([P, K], U8, name="wq_plane", align_bytes=64)
-        draft_plane = sb.tile([P, U], U8, name="draft_plane", align_bytes=64)
+        draft_plane = sb.tile([P, PIECE], U8, name="draft_plane", align_bytes=64)
         arch_plane = sb.tile([P, X], U8, name="arch_plane", align_bytes=64)
         cache_plane = sb.tile([P, T], U8, name="cache_plane", align_bytes=64)
         for plane in (wq_plane, draft_plane, cache_plane, arch_plane):
-            nc.gpsimd.memset(plane[:].bitcast(I32), 0)
+            nc.vector.memset(plane[:].bitcast(I32), 0)
         f1 = sb.tile([P, T], F32, name="f1")
-        nc.gpsimd.memset(f1[:], 0.0)
+        nc.vector.memset(f1[:], 0.0)
 
         s_raw = sb.tile([P, PACK, Q], F32, name="s_raw", align_bytes=256)
-        wq_raw = sb.tile([P, K], U32, name="wq_raw", tag="wq_raw_f2", align_bytes=256)
+        wq_raw = sb.tile([P, K], U32, name="wq_raw", align_bytes=256)
         draft_w = sb.tile([P, U], I32, name="draft_w", align_bytes=256)
         arch_w = sb.tile([P, 2 * X], U8, name="arch_w", align_bytes=256)
-        cache_w = sb.tile([P, 2 * T], U8, name="cache_w", align_bytes=256)
+        cache_w = sb.tile([P, 2 * T], U8, name="cache_w", tag="cache_w", align_bytes=256)
         lists = [sb.tile([P, I // 16], U16, name="list%d" % n) for n in range(6)]
         l1, l2, l3, l4, l5, l6 = lists
 
-        wq_stage = sb.tile([4, 4, K // 4], I32, name="wq_stage")
-        nc.sync.dma_start(wq_stage[:], wq_scales[0].bitcast(I32).rearrange("(g r) c -> r g c", r=4))
         nc.sync.dma_start(s_raw[:], states.rearrange("(p j) q -> p j q", j=PACK))
+        load_scale_rows(nc.sync, wq_plane, wq_scales)
         nc.sync.dma_start(wq_raw[:].bitcast(I32), wq_words[0].rearrange("p n t -> p (n t)").bitcast(I32))
-        load_scale_rows(nc, draft_plane, draft_scales)
         nc.sync.dma_start(draft_w[:], draft_words[0].rearrange("p n t -> p (n t)").bitcast(I32))
+        draft_rows = draft_scales[0].bitcast(I32)
+        for g in range(4):
+            nc.sync.dma_start(
+                draft_plane[32 * g : 32 * g + 16, :].bitcast(I32),
+                draft_rows[4 * g : 4 * g + 4, :].rearrange("r (n c) -> n r c", n=4),
+            )
         nc.sync.dma_start(l1[:], offs)
         nc.sync.dma_start(l2[:], offs2)
-        load_scale_rows(nc, cache_plane, cache_scales)
+        load_scale_rows(nc.sync, cache_plane, cache_scales)
         nc.sync.dma_start(cache_w[:].bitcast(I32), cache_words[0].bitcast(I32))
         nc.sync.dma_start(l4[:], offs4)
         nc.sync.dma_start(l3[:], offs3)
-        load_scale_rows(nc, arch_plane, arch_scales)
+        load_scale_rows(nc.sync, arch_plane, arch_scales)
         nc.sync.dma_start(arch_w[:].bitcast(I32), arch_words[0].bitcast(I32))
         nc.sync.dma_start(l5[:], offs5)
         nc.sync.dma_start(l6[:], offs6)
@@ -81,8 +85,6 @@ def tile_attend_gatedpage_sidethree_kernel(
             s_raw[:].rearrange("p j (c i) -> p c j i", i=4),
             COPY,
         )
-        for g in range(4):
-            nc.vector.tensor_copy(wq_plane[32 * g : 32 * g + 4, :].bitcast(I32), wq_stage[:, g, :])
         wq_deal_plane = sb.tile([P, K], U8, name="wq_deal_plane", align_bytes=64)
         nc.vector.tensor_copy(
             wq_deal_plane[:].rearrange("p (t m) -> p t m", t=PACK),
@@ -92,35 +94,35 @@ def tile_attend_gatedpage_sidethree_kernel(
         s_plane = sb.tile([P, Q], U8, name="s_plane", align_bytes=64)
         nc.vector.quantize_mx(s_codes[:].bitcast(FP8X4), s_plane[:], s_bf[:].rearrange("p q j -> p (q j)"))
         wq_deal = sb.tile([P, K], U32, name="wq_deal", align_bytes=64)
-        nc.scalar.copy(
-            wq_deal[:].rearrange("p (t c i) -> p c t i", t=PACK, i=4),
-            wq_raw[:].rearrange("p (c i t) -> p c t i", t=PACK, i=4),
-        )
+        dealt = wq_deal[:].rearrange("p (t c i) -> p c t i", t=PACK, i=4)
+        undealt = wq_raw[:].rearrange("p (c i t) -> p c t i", t=PACK, i=4)
+        nc.scalar.copy(dealt[:, :, 0:2, :], undealt[:, :, 0:2, :])
+        dealt_i = wq_deal[:].bitcast(I32).rearrange("p (t c i) -> p c t i", t=PACK, i=4)
+        undealt_i = wq_raw[:].bitcast(I32).rearrange("p (c i t) -> p c t i", t=PACK, i=4)
+        nc.vector.tensor_copy(dealt_i[:, :, 2:4, :], undealt_i[:, :, 2:4, :])
 
-        f2 = sb.tile([P, X], F32, name="f2", tag="wq_raw_f2", align_bytes=256)
-        nc.vector.memset(f2[:], 0.0)
-
-        qv_ps = ps.tile([P, PACK, Q], F32, name="qv_ps", tag="first")
+        qv_ps = [ps.tile([P, 2, Q], F32, name="qv_ps%d" % u) for u in range(2)]
         for t in range(PACK):
             cols = slice(t * P, (t + 1) * P)
             nc.tensor.matmul_mx(
-                qv_ps[:, t, :], lhsT=wq_deal[:, cols].bitcast(FP8X4), lhsT_scale=wq_deal_plane[:, cols],
+                qv_ps[t // 2][:, t % 2, :], lhsT=wq_deal[:, cols].bitcast(FP8X4), lhsT_scale=wq_deal_plane[:, cols],
                 rhs=s_codes[:].bitcast(FP8X4), rhs_scale=s_plane[:], start=True, stop=True,
             )
 
         q_bf = sb.tile([P, Q, PACK], BF16, name="q_bf", align_bytes=64)
-        nc.scalar.activation(q_bf[:], qv_ps[:].rearrange("p t q -> p q t"), COPY)
+        nc.vector.tensor_copy(q_bf[:, :, 0:2], qv_ps[0][:].rearrange("p t q -> p q t"))
+        nc.scalar.activation(q_bf[:, :, 2:4], qv_ps[1][:].rearrange("p t q -> p q t"), COPY)
         q_codes = sb.tile([P, Q], U32, name="q_codes", align_bytes=64)
         q_plane = sb.tile([P, Q], U8, name="q_plane", align_bytes=64)
         nc.vector.quantize_mx(q_codes[:].bitcast(FP8X4), q_plane[:], q_bf[:].rearrange("p q t -> p (q t)"))
 
-        b = sb.tile([P, U], F32, name="b")
+        b = sb.tile([P, U], F32, name="b", tag="b")
         for n in range(U // PIECE):
             cols = slice(n * PIECE, (n + 1) * PIECE)
             b_ps = ps.tile([P, PIECE], F32, name="b_ps%d" % n, tag="b%d" % n)
             nc.tensor.matmul_mx(
                 b_ps[:], lhsT=q_codes[:].bitcast(FP8X4), lhsT_scale=q_plane[:],
-                rhs=draft_w[:, cols].bitcast(FP8X4), rhs_scale=draft_plane[:, cols], start=True, stop=True,
+                rhs=draft_w[:, cols].bitcast(FP8X4), rhs_scale=draft_plane[4 * n : P, :], start=True, stop=True,
             )
             if n % 2 == 0:
                 nc.scalar.activation(b[:, cols], b_ps[:], COPY)
@@ -148,15 +150,20 @@ def tile_attend_gatedpage_sidethree_kernel(
         halves = [(slice(h * HALF, (h + 1) * HALF), slice(h * LCOL, (h + 1) * LCOL)) for h in range(2)]
 
         b1 = sb.tile([P, I], F32, name="b1")
-        for slots, lc in halves:
-            nc.vector.tensor_copy(b1[:, slots], b[:].indirect(l1[:, lc]))
-            nc.scalar.activation(f1[:].indirect(l2[:, lc]), b1[:, slots], COPY)
+        (lo, lo_lc), (hi, hi_lc) = halves
+        nc.vector.tensor_copy(b1[:, lo], b[:].indirect(l1[:, lo_lc]))
+        nc.scalar.activation(b1[:, hi], b[:].indirect(l1[:, hi_lc]), COPY)
+        nc.scalar.activation(f1[:].indirect(l2[:]), b1[:], COPY)
 
         a_half = sb.tile([P, T], F32, name="a_half")
         for n, bank in enumerate(a_ps):
             nc.vector.tensor_scalar(a_half[:, n * BANK : (n + 1) * BANK], bank[:], 0.5, None, ALU.mult)
         b4 = sb.tile([P, I], F32, name="b4")
         nc.vector.tensor_copy(b4[:], b[:].indirect(l4[:]))
+        f2b = sb.tile([P, X], F32, name="f2b", tag="cache_w", align_bytes=256)
+        nc.gpsimd.memset(f2b[:], 0.0)
+        f2a = sb.tile([P, X], F32, name="f2a", tag="b")
+        nc.gpsimd.memset(f2a[:], 0.0)
 
         th = sb.tile([P, T], F32, name="th")
         mg = sb.tile([P, T], F32, name="mg")
@@ -165,24 +172,26 @@ def tile_attend_gatedpage_sidethree_kernel(
             nc.scalar.activation(th[:, cols], f1[:, cols], TANH)
             nc.vector.scalar_tensor_tensor(mg[:, cols], th[:, cols], 1.0, a_half[:, cols], ALU.add, ALU.mult)
 
-        m3_lo = sb.tile([P, HALF], F32, name="m3_lo")
-        m3 = [m3_lo[:], b4[:, 0:HALF]]
+        m3 = sb.tile([P, I], F32, name="m3")
         w = sb.tile([P, I], F32, name="w")
-        for (slots, lc), m3_h in zip(halves, m3):
-            nc.vector.tensor_copy(m3_h, mg[:].indirect(l3[:, lc]))
-            nc.vector.tensor_tensor(w[:, slots], m3_h, b4[:, slots], ALU.max)
-            nc.scalar.activation(f2[:].indirect(l5[:, lc]), w[:, slots], COPY)
+        nc.vector.tensor_copy(m3[:, lo], mg[:].indirect(l3[:, lo_lc]))
+        nc.scalar.activation(m3[:, hi], mg[:].indirect(l3[:, hi_lc]), COPY)
+        for first, last, window in ((0, 128, f2a), (128, 256, f2b), (256, 512, f2a)):
+            slots = slice(first, last)
+            nc.vector.tensor_tensor(w[:, slots], m3[:, slots], b4[:, slots], ALU.max)
+            nc.scalar.activation(window[:].indirect(l5[:, first // 16 : last // 16]), w[:, slots], COPY)
 
-        cc = sb.tile([P, X], F32, name="cc")
+        cc_part = sb.tile([P, X], F32, name="cc_part")
         for n, bank in enumerate(c0_ps):
             cols = slice(n * BANK, (n + 1) * BANK)
-            nc.vector.tensor_tensor(cc[:, cols], bank[:], f2[:, cols], ALU.subtract)
+            nc.vector.tensor_tensor(cc_part[:, cols], bank[:], f2b[:, cols], ALU.subtract)
+        cc = sb.tile([P, X], F32, name="cc")
+        nc.vector.tensor_tensor(cc[:], cc_part[:], f2a[:], ALU.subtract)
 
         y = sb.tile([P, I], F32, name="y", align_bytes=256)
         c6 = sb.tile([P, HALF], F32, name="c6")
-        (lo, lo_lc), (hi, hi_lc) = halves
         nc.scalar.activation(c6[:], cc[:].indirect(l6[:, hi_lc]), COPY)
-        nc.vector.tensor_tensor(y[:, lo], cc[:].indirect(l6[:, lo_lc]), m3[0], ALU.add)
+        nc.vector.tensor_tensor(y[:, lo], cc[:].indirect(l6[:, lo_lc]), m3[:, lo], ALU.add)
         nc.sync.dma_start(out[:, lo], y[:, lo])
-        nc.vector.tensor_tensor(y[:, hi], c6[:], m3[1], ALU.add)
+        nc.vector.tensor_tensor(y[:, hi], c6[:], m3[:, hi], ALU.add)
         nc.scalar.dma_start(out[:, hi], y[:, hi])

from contextlib import ExitStack

import concourse.mybir as mybir

D, K, T, U, X, I, Q = 512, 512, 1024, 1024, 1024, 512, 128
FLOPS = 2 * (D * K * Q + K * Q * T + K * Q * U + D * Q * X)

F32 = mybir.dt.float32
BF16 = mybir.dt.bfloat16
I32 = mybir.dt.int32
U32 = mybir.dt.uint32
U16 = mybir.dt.uint16
U8 = mybir.dt.uint8
FP8X4 = mybir.dt.float8_e4m3fn_x4
FP4X4 = mybir.dt.float4_e2m1fn_x4
COPY = mybir.ActivationFunctionType.Copy
TANH = mybir.ActivationFunctionType.Tanh
ALU = mybir.AluOpType

P = 128
PACK = 4
BANK = 512
PIECE = 256
HALF = I // 2
LCOL = HALF // 16


def load_scale_rows(queue, plane, scales):
    rows = scales[0].bitcast(I32)
    words = plane[:].bitcast(I32)
    for r in range(4):
        queue.dma_start(words[r:P:32, :], rows[r:16:4, :])


def tile_attend_gatedpage_sidethree_kernel(
    tc, states, wq_words, wq_scales, cache_words, cache_scales, draft_words, draft_scales,
    arch_words, arch_scales, offs, offs2, offs3, offs4, offs5, offs6, out,
):
    nc = tc.nc
    with ExitStack() as ctx:
        sb = ctx.enter_context(tc.tile_pool(name="sb", bufs=1))
        ps = ctx.enter_context(tc.psum_pool(name="ps", bufs=1))

        wq_plane = sb.tile([P, K], U8, name="wq_plane", align_bytes=64)
        draft_plane = sb.tile([P, PIECE], U8, name="draft_plane", align_bytes=64)
        arch_plane = sb.tile([P, X], U8, name="arch_plane", align_bytes=64)
        cache_plane = sb.tile([P, T], U8, name="cache_plane", align_bytes=64)
        for plane in (wq_plane, draft_plane, cache_plane, arch_plane):
            nc.vector.memset(plane[:].bitcast(I32), 0)
        f1 = sb.tile([P, T], F32, name="f1")
        nc.vector.memset(f1[:], 0.0)

        s_raw = sb.tile([P, PACK, Q], F32, name="s_raw", align_bytes=256)
        wq_raw = sb.tile([P, K], U32, name="wq_raw", align_bytes=256)
        draft_w = sb.tile([P, U], I32, name="draft_w", align_bytes=256)
        arch_w = sb.tile([P, 2 * X], U8, name="arch_w", align_bytes=256)
        cache_w = sb.tile([P, 2 * T], U8, name="cache_w", tag="cache_w", align_bytes=256)
        lists = [sb.tile([P, I // 16], U16, name="list%d" % n) for n in range(6)]
        l1, l2, l3, l4, l5, l6 = lists

        nc.sync.dma_start(s_raw[:], states.rearrange("(p j) q -> p j q", j=PACK))
        load_scale_rows(nc.sync, wq_plane, wq_scales)
        nc.sync.dma_start(wq_raw[:].bitcast(I32), wq_words[0].rearrange("p n t -> p (n t)").bitcast(I32))
        nc.sync.dma_start(draft_w[:], draft_words[0].rearrange("p n t -> p (n t)").bitcast(I32))
        draft_rows = draft_scales[0].bitcast(I32)
        for g in range(4):
            nc.sync.dma_start(
                draft_plane[32 * g : 32 * g + 16, :].bitcast(I32),
                draft_rows[4 * g : 4 * g + 4, :].rearrange("r (n c) -> n r c", n=4),
            )
        nc.sync.dma_start(l1[:], offs)
        nc.sync.dma_start(l2[:], offs2)
        load_scale_rows(nc.sync, cache_plane, cache_scales)
        nc.sync.dma_start(cache_w[:].bitcast(I32), cache_words[0].bitcast(I32))
        nc.sync.dma_start(l4[:], offs4)
        nc.sync.dma_start(l3[:], offs3)
        load_scale_rows(nc.sync, arch_plane, arch_scales)
        nc.sync.dma_start(arch_w[:].bitcast(I32), arch_words[0].bitcast(I32))
        nc.sync.dma_start(l5[:], offs5)
        nc.sync.dma_start(l6[:], offs6)

        s_bf = sb.tile([P, Q, PACK], BF16, name="s_bf", align_bytes=64)
        nc.scalar.activation(
            s_bf[:].rearrange("p (c i) j -> p c j i", i=4),
            s_raw[:].rearrange("p j (c i) -> p c j i", i=4),
            COPY,
        )
        wq_deal_plane = sb.tile([P, K], U8, name="wq_deal_plane", align_bytes=64)
        nc.vector.tensor_copy(
            wq_deal_plane[:].rearrange("p (t m) -> p t m", t=PACK),
            wq_plane[:].rearrange("p (m t) -> p t m", t=PACK),
        )
        s_codes = sb.tile([P, Q], U32, name="s_codes", align_bytes=64)
        s_plane = sb.tile([P, Q], U8, name="s_plane", align_bytes=64)
        nc.vector.quantize_mx(s_codes[:].bitcast(FP8X4), s_plane[:], s_bf[:].rearrange("p q j -> p (q j)"))
        wq_deal = sb.tile([P, K], U32, name="wq_deal", align_bytes=64)
        dealt = wq_deal[:].rearrange("p (t c i) -> p c t i", t=PACK, i=4)
        undealt = wq_raw[:].rearrange("p (c i t) -> p c t i", t=PACK, i=4)
        nc.scalar.copy(dealt[:, :, 0:2, :], undealt[:, :, 0:2, :])
        dealt_i = wq_deal[:].bitcast(I32).rearrange("p (t c i) -> p c t i", t=PACK, i=4)
        undealt_i = wq_raw[:].bitcast(I32).rearrange("p (c i t) -> p c t i", t=PACK, i=4)
        nc.vector.tensor_copy(dealt_i[:, :, 2:4, :], undealt_i[:, :, 2:4, :])

        qv_ps = [ps.tile([P, 2, Q], F32, name="qv_ps%d" % u) for u in range(2)]
        for t in range(PACK):
            cols = slice(t * P, (t + 1) * P)
            nc.tensor.matmul_mx(
                qv_ps[t // 2][:, t % 2, :], lhsT=wq_deal[:, cols].bitcast(FP8X4), lhsT_scale=wq_deal_plane[:, cols],
                rhs=s_codes[:].bitcast(FP8X4), rhs_scale=s_plane[:], start=True, stop=True,
            )

        q_bf = sb.tile([P, Q, PACK], BF16, name="q_bf", align_bytes=64)
        nc.vector.tensor_copy(q_bf[:, :, 0:2], qv_ps[0][:].rearrange("p t q -> p q t"))
        nc.scalar.activation(q_bf[:, :, 2:4], qv_ps[1][:].rearrange("p t q -> p q t"), COPY)
        q_codes = sb.tile([P, Q], U32, name="q_codes", align_bytes=64)
        q_plane = sb.tile([P, Q], U8, name="q_plane", align_bytes=64)
        nc.vector.quantize_mx(q_codes[:].bitcast(FP8X4), q_plane[:], q_bf[:].rearrange("p q t -> p (q t)"))

        b = sb.tile([P, U], F32, name="b", tag="b")
        for n in range(U // PIECE):
            cols = slice(n * PIECE, (n + 1) * PIECE)
            b_ps = ps.tile([P, PIECE], F32, name="b_ps%d" % n, tag="b%d" % n)
            nc.tensor.matmul_mx(
                b_ps[:], lhsT=q_codes[:].bitcast(FP8X4), lhsT_scale=q_plane[:],
                rhs=draft_w[:, cols].bitcast(FP8X4), rhs_scale=draft_plane[4 * n : P, :], start=True, stop=True,
            )
            if n % 2 == 0:
                nc.scalar.activation(b[:, cols], b_ps[:], COPY)
            else:
                nc.vector.tensor_copy(b[:, cols], b_ps[:])
        a_ps = [
            ps.tile([P, BANK], F32, name="a_ps0", tag="b1"),
            ps.tile([P, BANK], F32, name="a_ps1", tag="b3"),
        ]
        for n, bank in enumerate(a_ps):
            nc.tensor.matmul_mx(
                bank[:], lhsT=q_codes[:].bitcast(FP8X4), lhsT_scale=q_plane[:],
                rhs=cache_w[:, 2 * n * BANK : 2 * (n + 1) * BANK].bitcast(FP4X4),
                rhs_scale=cache_plane[:, n * BANK : (n + 1) * BANK], start=True, stop=True,
            )

        c0_ps = [ps.tile([P, BANK], F32, name="c0_ps%d" % n) for n in range(X // BANK)]
        for n, bank in enumerate(c0_ps):
            nc.tensor.matmul_mx(
                bank[:], lhsT=s_codes[:].bitcast(FP8X4), lhsT_scale=s_plane[:],
                rhs=arch_w[:, 2 * n * BANK : 2 * (n + 1) * BANK].bitcast(FP4X4),
                rhs_scale=arch_plane[:, n * BANK : (n + 1) * BANK], start=True, stop=True,
            )

        halves = [(slice(h * HALF, (h + 1) * HALF), slice(h * LCOL, (h + 1) * LCOL)) for h in range(2)]

        b1 = sb.tile([P, I], F32, name="b1")
        (lo, lo_lc), (hi, hi_lc) = halves
        nc.vector.tensor_copy(b1[:, lo], b[:].indirect(l1[:, lo_lc]))
        nc.scalar.activation(b1[:, hi], b[:].indirect(l1[:, hi_lc]), COPY)
        nc.scalar.activation(f1[:].indirect(l2[:]), b1[:], COPY)

        a_half = sb.tile([P, T], F32, name="a_half")
        for n, bank in enumerate(a_ps):
            nc.vector.tensor_scalar(a_half[:, n * BANK : (n + 1) * BANK], bank[:], 0.5, None, ALU.mult)
        b4 = sb.tile([P, I], F32, name="b4")
        nc.vector.tensor_copy(b4[:], b[:].indirect(l4[:]))
        f2b = sb.tile([P, X], F32, name="f2b", tag="cache_w", align_bytes=256)
        nc.gpsimd.memset(f2b[:], 0.0)
        f2a = sb.tile([P, X], F32, name="f2a", tag="b")
        nc.gpsimd.memset(f2a[:], 0.0)

        th = sb.tile([P, T], F32, name="th")
        mg = sb.tile([P, T], F32, name="mg")
        for n in range(T // PIECE):
            cols = slice(n * PIECE, (n + 1) * PIECE)
            nc.scalar.activation(th[:, cols], f1[:, cols], TANH)
            nc.vector.scalar_tensor_tensor(mg[:, cols], th[:, cols], 1.0, a_half[:, cols], ALU.add, ALU.mult)

        m3 = sb.tile([P, I], F32, name="m3")
        w = sb.tile([P, I], F32, name="w")
        nc.vector.tensor_copy(m3[:, lo], mg[:].indirect(l3[:, lo_lc]))
        nc.scalar.activation(m3[:, hi], mg[:].indirect(l3[:, hi_lc]), COPY)
        for first, last, window in ((0, 128, f2a), (128, 256, f2b), (256, 512, f2a)):
            slots = slice(first, last)
            nc.vector.tensor_tensor(w[:, slots], m3[:, slots], b4[:, slots], ALU.max)
            nc.scalar.activation(window[:].indirect(l5[:, first // 16 : last // 16]), w[:, slots], COPY)

        cc_part = sb.tile([P, X], F32, name="cc_part")
        for n, bank in enumerate(c0_ps):
            cols = slice(n * BANK, (n + 1) * BANK)
            nc.vector.tensor_tensor(cc_part[:, cols], bank[:], f2b[:, cols], ALU.subtract)
        cc = sb.tile([P, X], F32, name="cc")
        nc.vector.tensor_tensor(cc[:], cc_part[:], f2a[:], ALU.subtract)

        y = sb.tile([P, I], F32, name="y", align_bytes=256)
        c6 = sb.tile([P, HALF], F32, name="c6")
        nc.scalar.activation(c6[:], cc[:].indirect(l6[:, hi_lc]), COPY)
        nc.vector.tensor_tensor(y[:, lo], cc[:].indirect(l6[:, lo_lc]), m3[:, lo], ALU.add)
        nc.sync.dma_start(out[:, lo], y[:, lo])
        nc.vector.tensor_tensor(y[:, hi], c6[:], m3[:, hi], ALU.add)
        nc.scalar.dma_start(out[:, hi], y[:, hi])
